import numpy as np
import ml_dtypes


def mxq(x, axis, fmt="e4m3"):
    dtype, down = {"e4m3": (ml_dtypes.float8_e4m3fn, 7), "e5m2": (ml_dtypes.float8_e5m2, 14)}[fmt]
    v = np.moveaxis(np.asarray(x, np.float32).astype(ml_dtypes.bfloat16).astype(np.float64), axis, -1)
    blocks = v.reshape(v.shape[:-1] + (-1, 32))
    amax = np.abs(blocks).max(-1, keepdims=True)
    byte = np.maximum(np.where(amax > 0, np.frexp(amax)[1] - 1 + 127, 0) - down, 1)
    scale = np.exp2(byte - 127.0)
    codes = (blocks / scale).astype(np.float32).astype(dtype).astype(np.float64)
    return np.moveaxis((codes * scale).reshape(v.shape), -1, axis)


WIDE = False


def mx_kscale(k):
    if not WIDE:
        return np.ones(k)
    levels = np.array([10, -10, 5, -5, 0])
    if k % 512:
        return np.exp2(np.random.permutation(np.resize(levels, k // 32))).repeat(32)
    a = np.empty((k // 512, 16))
    for p in range(k // 512):
        a[p, :8] = np.random.permutation(np.resize(levels, 8))
        for g in range(8):
            far = levels[np.abs(levels - a[p, g]) >= 10]
            a[p, g + 8] = far[np.random.randint(len(far))]
    return np.exp2(a.ravel()).repeat(32)


def f64(x):
    return np.asarray(x).astype(np.float64)


def striped8(idx):
    return np.asarray(idx).reshape(8, -1, 16).transpose(0, 2, 1).reshape(128, -1).astype(np.uint16)


def unstriped8(offs):
    return offs.reshape(8, 16, -1).transpose(0, 2, 1).reshape(8, -1).astype(np.int64)


def pick8(x, idx, run):
    r = np.arange(len(x))
    return x[r[:, None], idx[r % (8 * run) // run]]


E2M1 = np.array([0.0, 0.5, 1.0, 1.5, 2.0, 3.0, 4.0, 6.0, -0.0, -0.5, -1.0, -1.5, -2.0, -3.0, -4.0, -6.0])


def pack_weight(w, fmt):
    k, n = w.shape
    w = f64(np.asarray(w, np.float32).astype(ml_dtypes.bfloat16)).reshape(k // 32, 32, n)
    amax = np.abs(w).max(1)
    if fmt == "e4m3":
        byte = np.frexp(amax)[1] - 1 + 127 - 7
    else:
        mant, ex = np.frexp(amax / 6.0)
        byte = np.where(mant > 0.5, ex, ex - 1) + 127
    byte = np.clip(np.where(amax > 0, byte, 1), 1, 254)
    scaled = (w * np.exp2(127.0 - byte)[:, None, :]).reshape(k, n).astype(np.float32)
    by_word = np.ascontiguousarray(scaled.reshape(k // 512, 128, 4, n).transpose(0, 1, 3, 2))
    if fmt == "e4m3":
        words = by_word.astype(ml_dtypes.float8_e4m3fn).view(np.uint8)
    else:
        c = by_word.astype(ml_dtypes.float4_e2m1fn).view(np.uint8) & 0xF
        words = (c[..., 0::2] | (c[..., 1::2] << 4)).reshape(k // 512, 128, 2 * n)
    return np.ascontiguousarray(words), np.ascontiguousarray(byte.astype(np.uint8).reshape(k // 512, 16, n))


def unpack_weight(words, scales, fmt):
    g, _, n = scales.shape
    words = np.ascontiguousarray(words).reshape(g, 128, n, -1)
    if fmt == "e4m3":
        vals = words.view(ml_dtypes.float8_e4m3fn).astype(np.float64)
    else:
        nib = np.empty((g, 128, n, 4), np.uint8)
        nib[..., 0::2] = words & 0xF
        nib[..., 1::2] = words >> 4
        vals = E2M1[nib]
    vals = vals * np.repeat(np.exp2(scales.astype(np.float64) - 127.0), 8, axis=1)[..., None]
    return vals.transpose(0, 1, 3, 2).reshape(g * 512, n)


D, V, Q, I = 512, 2048, 128, 512


def setup_inputs():
    n = np.random.standard_normal
    idx = np.stack([np.random.permutation(V)[:I] for _ in range(8)])
    idx2 = np.stack([np.random.permutation(V)[:I] for _ in range(8)])
    fd = mx_kscale(D)
    vocp = pack_weight(n((D, V)) / fd[:, None], "e4m3")
    return {
        "hid": (n((D, Q)) * 1.0 / np.sqrt(D) * fd[:, None]).astype(np.float32),
        "voc_words": vocp[0],
        "voc_scales": vocp[1],
        "stake": (np.random.uniform(0.5, 2.0, (Q, 1))).astype(np.float32),
        "dhid": (n((D, Q)) * 1.0 / np.sqrt(D) * fd[:, None]).astype(np.float32),
        "base": (0.5 * n((Q, V))).astype(np.float32),
        "offs": striped8(idx),
        "offs2": striped8(idx2),
    }


def reference(hid, voc_words, voc_scales, stake, dhid, base, offs, offs2):
    idx = unstriped8(offs)
    idx2 = unstriped8(offs2)
    vocu = unpack_weight(voc_words, voc_scales, "e4m3")
    hidq = mxq(f64(hid), 0, "e4m3")
    a = hidq.T @ vocu
    dhidq = mxq(f64(dhid), 0, "e4m3")
    ta = dhidq.T @ vocu
    m1 = np.max(a, axis=1, keepdims=True)
    p = np.exp(a - m1)
    z = np.sum(p, axis=1, keepdims=True)
    px = np.exp(pick8(a, idx, 16) - m1)
    px2 = np.exp(pick8(a, idx2, 16) - m1)
    ma = np.sum(px, axis=1, keepdims=True) / z
    mb = np.sum(px2, axis=1, keepdims=True) / z
    dmb = f64(stake) / (ma * mb * 16.0 + 1.0) * 16.0 * ma
    dma = f64(stake) / (ma * mb * 16.0 + 1.0) * 16.0 * mb
    dpx2 = dmb / z
    dpx = dma / z
    dz = dmb * np.sum(px2, axis=1, keepdims=True) / np.square(z) * (-1.0) - dma * np.sum(px, axis=1, keepdims=True) / np.square(z)
    xp = ta * p
    xz = np.sum(xp, axis=1, keepdims=True)
    xpx = pick8(ta, idx, 16) * px
    xpx2 = pick8(ta, idx2, 16) * px2
    xma = (np.sum(xpx, axis=1, keepdims=True) - xz * np.sum(px, axis=1, keepdims=True) / z) / z
    xmb = (np.sum(xpx2, axis=1, keepdims=True) - xz * np.sum(px2, axis=1, keepdims=True) / z) / z
    xdmb = (xma * mb + xmb * ma) * 16.0 * f64(stake) / np.square(ma * mb * 16.0 + 1.0) * (-1.0) * 16.0 * ma + xma * f64(stake) / (ma * mb * 16.0 + 1.0) * 16.0
    xdma = (xma * mb + xmb * ma) * 16.0 * f64(stake) / np.square(ma * mb * 16.0 + 1.0) * (-1.0) * 16.0 * mb + xmb * f64(stake) / (ma * mb * 16.0 + 1.0) * 16.0
    xdpx2 = (xdmb - xz * dmb / z) / z
    xdpx = (xdma - xz * dma / z) / z
    xdz = (xdmb * np.sum(px2, axis=1, keepdims=True) + np.sum(xpx2, axis=1, keepdims=True) * dmb - xz * z * 2.0 * dmb * np.sum(px2, axis=1, keepdims=True) / np.square(z)) / np.square(z) * (-1.0) - (xdma * np.sum(px, axis=1, keepdims=True) + np.sum(xpx, axis=1, keepdims=True) * dma - xz * z * 2.0 * dma * np.sum(px, axis=1, keepdims=True) / np.square(z)) / np.square(z)
    xe1 = xdpx2 * px2 + xpx2 * dpx2
    xs1 = np.zeros((Q, V))
    xs1[np.arange(Q)[:, None], idx2[np.arange(Q) % 128 // 16]] = xe1
    xe2 = xdpx * px + xpx * dpx
    xs2 = np.zeros((Q, V))
    xs2[np.arange(Q)[:, None], idx[np.arange(Q) % 128 // 16]] = xe2
    xda = xdz * p + xp * dz + xs1 + xs2
    y = xda * 512.0 + f64(base)
    return y

@@ -1,0 +1,223 @@
+from contextlib import ExitStack
+
+import concourse.mybir as mybir
+from concourse.masks import make_identity
+
+F32 = mybir.dt.float32
+BF16 = mybir.dt.bfloat16
+I32 = mybir.dt.int32
+U32 = mybir.dt.uint32
+U16 = mybir.dt.uint16
+U8 = mybir.dt.uint8
+FP8X4 = mybir.dt.float8_e4m3fn_x4
+ALU = mybir.AluOpType
+ACT = mybir.ActivationFunctionType
+AXIS = mybir.AxisListType
+
+P = 128
+D, V, Q, LISTED = 512, 2048, 128, 512
+PACK = 4
+BANK = 512
+CHUNKS = V // BANK
+BLOCKS = BANK // P
+
+FLOPS = 2 * 2 * D * Q * V
+
+
+def tile_attend_hvjointcover_heads_kernel(tc, hid, voc_words, voc_scales, stake, dhid, base, offs, offs2, out):
+    nc = tc.nc
+    mult, add = ALU.mult, ALU.add
+
+    with ExitStack() as ctx:
+        keep = ctx.enter_context(tc.tile_pool(name="keep", bufs=1))
+        psum = ctx.enter_context(tc.psum_pool(name="psum", bufs=1))
+
+        def chunk(c):
+            return slice(c * BANK, (c + 1) * BANK)
+
+        def block(b):
+            return slice(b * P, (b + 1) * P)
+
+        def column(name, width=1):
+            return keep.tile([P, width], F32, name=name)
+
+        planes = keep.tile([P, BANK], U8, name="planes", align_bytes=64)
+        nc.vector.memset(planes[:].bitcast(I32), 0)
+
+        hid_raw = keep.tile([P, PACK, Q], F32, name="hid_raw")
+        nc.sync.dma_start(out=hid_raw[:], in_=hid.rearrange("(p t) q -> p t q", t=PACK))
+        dhid_raw = keep.tile([P, PACK, Q], F32, name="dhid_raw")
+        nc.sync.dma_start(out=dhid_raw[:], in_=dhid.rearrange("(p t) q -> p t q", t=PACK))
+        for quad in range(4):
+            nc.sync.dma_start(
+                out=planes[32 * quad : 32 * quad + 16, :].bitcast(I32),
+                in_=voc_scales[0][4 * quad : 4 * quad + 4, :].bitcast(I32).rearrange("r (c n) -> c r n", c=CHUNKS),
+            )
+        words_hbm = voc_words[0].rearrange("p n t -> p (n t)")
+        words = [keep.tile([P, BANK], U32, name="words%d" % c, align_bytes=64) for c in range(CHUNKS)]
+        for c in range(CHUNKS):
+            nc.sync.dma_start(
+                out=words[c][:].bitcast(I32),
+                in_=words_hbm[:, PACK * c * BANK : PACK * (c + 1) * BANK].bitcast(I32),
+            )
+        list_a = keep.tile([P, LISTED // 16], U16, name="list_a")
+        list_b = keep.tile([P, LISTED // 16], U16, name="list_b")
+        nc.sync.dma_start(list_a[:], offs)
+        nc.sync.dma_start(list_b[:], offs2)
+        stake_sb = column("stake_sb")
+        nc.sync.dma_start(out=stake_sb[:], in_=stake)
+        base_sb = keep.tile([P, V], F32, name="base_sb")
+        nc.sync.dma_start(out=base_sb[:], in_=base)
+
+        warm = column("warm")
+        nc.vector.memset(warm[:], 0.0)
+        warm_out = column("warm_out")
+        nc.scalar.activation(warm_out[:], warm[:], ACT.Exp)
+        ident = keep.tile([P, P], F32, name="ident")
+        make_identity(nc, ident[:])
+        xs_a = keep.tile([P, V], F32, name="xs_a")
+        nc.vector.memset(xs_a[:], 0.0)
+
+        def quantise(raw, name, tag, cast):
+            grouped = keep.tile([P, Q, PACK], BF16, name=name + "_bf16", tag=tag, align_bytes=64)
+            cast(grouped[:], raw[:].rearrange("p t q -> p q t"))
+            codes = keep.tile([P, Q], U32, name=name + "_codes", align_bytes=64)
+            scales = keep.tile([P, Q], U8, name=name + "_scales", align_bytes=64)
+            nc.vector.quantize_mx(
+                out=codes[:].bitcast(FP8X4), scales=scales[:], in_=grouped[:].rearrange("p q t -> p (q t)")
+            )
+            return codes, scales
+
+        hid_mx = quantise(hid_raw, "hid", "hid_bf16", nc.vector.tensor_copy)
+        dhid_mx = quantise(dhid_raw, "dhid", "late", nc.scalar.copy)
+        xs_b = keep.tile([P, V], F32, name="xs_b", tag="late", align_bytes=64)
+        nc.gpsimd.memset(xs_b[:], 0.0)
+
+        a_sb = keep.tile([P, V], F32, name="a_sb")
+        ta_sb = keep.tile([P, V], F32, name="ta_sb")
+        chunk_max = column("chunk_max", CHUNKS)
+
+        def product(operand, c, tag):
+            bank = psum.tile([P, BANK], F32, name=tag + "_mx", tag=tag)
+            nc.tensor.matmul_mx(
+                out=bank[:],
+                lhsT=operand[0][:].bitcast(FP8X4),
+                lhsT_scale=operand[1][:],
+                rhs=words[c][:].bitcast(FP8X4),
+                rhs_scale=planes[4 * c : P, :],
+                start=True,
+                stop=True,
+            )
+            return bank
+
+        for c in range(CHUNKS):
+            a_bank = product(hid_mx, c, "first%d" % c)
+            nc.vector.tensor_scalar(
+                a_sb[:, chunk(c)], a_bank[:], 1.0, None, mult, ALU.max, accum_out=chunk_max[:, c : c + 1]
+            )
+            ta_bank = product(dhid_mx, c, "second%d" % c)
+            nc.scalar.copy(ta_sb[:, chunk(c)], ta_bank[:])
+
+        neg_max = column("neg_max")
+        nc.vector.tensor_reduce(neg_max[:], chunk_max[:], AXIS.X, ALU.max, negate=True)
+
+        def listed(name):
+            return keep.tile([P, LISTED], F32, name=name)
+
+        a_a, a_b, ta_a, ta_b = listed("a_a"), listed("a_b"), listed("ta_a"), listed("ta_b")
+        px_a, px_b = listed("px_a"), listed("px_b")
+        p = keep.tile([P, V], F32, name="p")
+        xp = keep.tile([P, V], F32, name="xp")
+        sums_f = column("sums_f", 4)
+        zq, s_b, s_a, s_ba = sums_f[:, 0:1], sums_f[:, 1:2], sums_f[:, 2:3], sums_f[:, 1:3]
+        KX = 2
+        ROW = KX + 2
+        xvec = column("xvec", ROW)
+        rows = keep.tile([P, 3, ROW], F32, name="rows")
+        flat = rows[:].rearrange("p r k -> p (r k)")
+        stake_k = column("stake_k", 2)
+        nc.vector.tensor_scalar(stake_k[:, 0:1], stake_sb[:], 512.0, None, mult)
+        nc.vector.tensor_scalar(stake_k[:, 1:2], stake_sb[:], 64.0, None, mult)
+
+        nc.vector.tensor_copy(a_a[:], a_sb[:].indirect(list_a[:]))
+        nc.vector.tensor_copy(a_b[:], a_sb[:].indirect(list_b[:]))
+        z = column("z")
+        nc.scalar.activation(p[:], a_sb[:], ACT.Exp, bias=neg_max[:], accum_out=z[:])
+        nc.scalar.activation(px_a[:], a_a[:], ACT.Exp, bias=neg_max[:], accum_out=s_a)
+        nc.scalar.activation(px_b[:], a_b[:], ACT.Exp, bias=neg_max[:], accum_out=s_b)
+        nc.vector.tensor_scalar(zq, z[:], 0.25, None, mult)
+        nc.vector.tensor_copy(ta_a[:], ta_sb[:].indirect(list_a[:]))
+        rq = column("rq")
+        nc.vector.reciprocal(rq[:], zq)
+        nc.vector.tensor_scalar(flat[:, KX + 1 : ROW + KX + 1 : KX + 1], zq.to_broadcast([P, 2]), zq, None, mult)
+        nc.vector.tensor_copy(ta_b[:], ta_sb[:].indirect(list_b[:]))
+        sums = [psum.tile([P, BANK], F32, name="sum%d" % c, tag="first%d" % c) for c in range(CHUNKS)]
+
+        def add_turned(source, c, first, last):
+            for b in range(BLOCKS):
+                nc.tensor.matmul(
+                    sums[c][:, block(b)],
+                    lhsT=source[:, block(b)],
+                    rhs=ident[:],
+                    start=(first and b == 0),
+                    stop=(last and b == BLOCKS - 1),
+                    is_transpose=True,
+                )
+
+        for c in range(CHUNKS):
+            add_turned(base_sb[:, chunk(c)], c, True, False)
+
+        prods = column("prods", 2)
+        norm = column("norm")
+        nc.vector.scalar_tensor_tensor(prods[:], sums_f[:, 0:3:2], 1.0, sums_f[:, 0:2], mult, mult, accum_out=norm[:])
+        s_ab = prods[:, 1:2]
+        nc.vector.tensor_scalar(rows[:, 0:2, 0:KX], s_ba.unsqueeze(2).to_broadcast([P, 2, KX]), zq, -0.5, mult, mult)
+        nc.vector.tensor_scalar(rows[:, 2, KX:ROW], s_ba, zq, -4.0, mult, mult)
+        nc.vector.scalar_tensor_tensor(flat[:, KX : ROW + KX + 2 : ROW + 1], s_ba, -1.0, s_ba, mult, mult)
+        nc.vector.scalar_tensor_tensor(xp[:, 0:1024], ta_sb[:, 0:1024], 1.0, p[:, 0:1024], mult, mult, accum_out=xvec[:, 0:1])
+        rn = column("rn")
+        nc.vector.reciprocal(rn[:], norm[:])
+        nc.vector.tensor_scalar(sums_f[:, 3:4], s_ab, rq[:], -0.5, mult, mult)
+        t16 = column("t16")
+        nc.vector.tensor_scalar(t16[:], s_ab, rq[:], rq[:], mult, mult)
+        nc.vector.scalar_tensor_tensor(xp[:, 1024:2048], ta_sb[:, 1024:2048], 1.0, p[:, 1024:2048], mult, mult, accum_out=xvec[:, 1:2])
+        slope = column("slope", 3)
+        nc.vector.tensor_scalar(slope[:], sums_f[:, 1:4], rn[:], stake_k[:, 0:1], mult, mult)
+        gain = column("gain", 2)
+        nc.vector.tensor_scalar(gain[:], stake_k[:], rn[:], rn[:], mult, mult)
+        nc.vector.tensor_scalar(rows[:, 2, 0:KX], t16[:].to_broadcast([P, KX]), 3.0, s_ab, add, mult)
+        xpx_a = listed("xpx_a")
+        nc.vector.scalar_tensor_tensor(xpx_a[:], ta_a[:], 1.0, px_a[:], mult, mult, accum_out=xvec[:, KX : KX + 1])
+        xpx_b = listed("xpx_b")
+        nc.vector.scalar_tensor_tensor(xpx_b[:], ta_b[:], 1.0, px_b[:], mult, mult, accum_out=xvec[:, KX + 1 : ROW])
+        offset = column("offset", 3)
+        terms = keep.tile([P, 3, ROW], F32, name="terms")
+        for k in range(3):
+            nc.vector.scalar_tensor_tensor(
+                terms[:, k, :], rows[:, k, :], gain[:, k // 2 : k // 2 + 1], xvec[:], mult, mult, accum_out=offset[:, k : k + 1]
+            )
+
+        u_a, u_b = listed("u_a"), listed("u_b")
+        nc.vector.tensor_scalar(u_a[:], ta_a[:], slope[:, 0:1], offset[:, 0:1], mult, add)
+        nc.vector.tensor_scalar(u_b[:], ta_b[:], slope[:, 1:2], offset[:, 1:2], mult, add)
+        nc.vector.tensor_tensor(xs_a[:].indirect(list_a[:]), u_a[:], px_a[:], mult)
+        nc.vector.tensor_tensor(xs_b[:].indirect(list_b[:]), u_b[:], px_b[:], mult)
+
+        term_xp = [keep.tile([P, BANK], F32, name="term_xp%d" % c) for c in range(CHUNKS)]
+        term_p = [keep.tile([P, BANK], F32, name="term_p%d" % c) for c in range(CHUNKS)]
+        for c in range(CHUNKS):
+            nc.scalar.activation(term_xp[c][:], xp[:, chunk(c)], ACT.Copy, scale=slope[:, 2:3])
+            add_turned(term_xp[c][:], c, False, False)
+        for c in range(CHUNKS):
+            nc.scalar.activation(term_p[c][:], p[:, chunk(c)], ACT.Copy, scale=offset[:, 2:3])
+            add_turned(term_p[c][:], c, False, False)
+        for c in range(CHUNKS):
+            add_turned(xs_a[:, chunk(c)], c, False, True)
+            turned = keep.tile([P, BANK], F32, name="turned%d" % c)
+            nc.scalar.copy(turned[:], sums[c][:])
+            upright = psum.tile([P, BANK], F32, name="upright%d" % c, tag="second%d" % c)
+            for b in range(BLOCKS):
+                nc.tensor.transpose(upright[:, block(b)], turned[:, block(b)], ident[:])
+            result = keep.tile([P, BANK], F32, name="result%d" % c)
+            nc.vector.tensor_tensor(result[:], upright[:], xs_b[:, chunk(c)], add)
+            nc.sync.dma_start(out=out[:, chunk(c)], in_=result[:])

@@ -110,13 +110,24 @@ def tile_attend_hvjointcover_heads_kernel(tc, hid, voc_words, voc_scales, stake,
             )
             return bank
 
-        for c in range(CHUNKS):
-            a_bank = product(hid_mx, c, "first%d" % c)
+        def score(c):
+            bank = product(hid_mx, c, "bank%d" % c)
             nc.vector.tensor_scalar(
-                a_sb[:, chunk(c)], a_bank[:], 1.0, None, mult, ALU.max, accum_out=chunk_max[:, c : c + 1]
+                a_sb[:, chunk(c)], bank[:], 1.0, None, mult, ALU.max, accum_out=chunk_max[:, c : c + 1]
             )
-            ta_bank = product(dhid_mx, c, "second%d" % c)
-            nc.scalar.copy(ta_sb[:, chunk(c)], ta_bank[:])
+
+        def tangent(c, tag):
+            bank = product(dhid_mx, c, tag)
+            nc.scalar.copy(ta_sb[:, chunk(c)], bank[:])
+
+        score(0)
+        tangent(0, "bank4")
+        score(1)
+        score(2)
+        score(3)
+        tangent(3, "bank5")
+        tangent(1, "bank2")
+        tangent(2, "bank3")
 
         neg_max = column("neg_max")
         nc.vector.tensor_reduce(neg_max[:], chunk_max[:], AXIS.X, ALU.max, negate=True)
@@ -128,30 +139,39 @@ def tile_attend_hvjointcover_heads_kernel(tc, hid, voc_words, voc_scales, stake,
         px_a, px_b = listed("px_a"), listed("px_b")
         p = keep.tile([P, V], F32, name="p")
         xp = keep.tile([P, V], F32, name="xp")
-        sums_f = column("sums_f", 4)
-        zq, s_b, s_a, s_ba = sums_f[:, 0:1], sums_f[:, 1:2], sums_f[:, 2:3], sums_f[:, 1:3]
+        listed_sums = column("listed_sums", 2)
+        s_b, s_a = listed_sums[:, 0:1], listed_sums[:, 1:2]
         KX = 2
         ROW = KX + 2
         xvec = column("xvec", ROW)
         rows = keep.tile([P, 3, ROW], F32, name="rows")
         flat = rows[:].rearrange("p r k -> p (r k)")
-        stake_k = column("stake_k", 2)
-        nc.vector.tensor_scalar(stake_k[:, 0:1], stake_sb[:], 512.0, None, mult)
-        nc.vector.tensor_scalar(stake_k[:, 1:2], stake_sb[:], 64.0, None, mult)
+        def scaled(dst, src, scale):
+            nc.scalar.activation(dst, src, ACT.Copy, scale=scale)
+
+        def affine(dst, src, scale, bias):
+            nc.scalar.activation(dst, src, ACT.Identity, scale=scale, bias=bias)
+
+        stake_k = column("stake_k", 3)
+        for k, factor in enumerate((512.0, -512.0, -256.0)):
+            scaled(stake_k[:, k : k + 1], stake_sb[:], factor)
+        divisors = column("divisors", 4)
+        norm, zq = divisors[:, 0:1], divisors[:, 3:4]
 
         nc.vector.tensor_copy(a_a[:], a_sb[:].indirect(list_a[:]))
         nc.vector.tensor_copy(a_b[:], a_sb[:].indirect(list_b[:]))
         z = column("z")
+        zs = column("zs", 3)
+        z_half, z_eighth, zq2 = zs[:, 0:1], zs[:, 1:2], zs[:, 2:3]
         nc.scalar.activation(p[:], a_sb[:], ACT.Exp, bias=neg_max[:], accum_out=z[:])
         nc.scalar.activation(px_a[:], a_a[:], ACT.Exp, bias=neg_max[:], accum_out=s_a)
+        nc.scalar.activation(zq2, z[:], ACT.Square, scale=0.25)
+        scaled(zq, z[:], 0.25)
         nc.scalar.activation(px_b[:], a_b[:], ACT.Exp, bias=neg_max[:], accum_out=s_b)
-        nc.vector.tensor_scalar(zq, z[:], 0.25, None, mult)
         nc.vector.tensor_copy(ta_a[:], ta_sb[:].indirect(list_a[:]))
-        rq = column("rq")
-        nc.vector.reciprocal(rq[:], zq)
-        nc.vector.tensor_scalar(flat[:, KX + 1 : ROW + KX + 1 : KX + 1], zq.to_broadcast([P, 2]), zq, None, mult)
         nc.vector.tensor_copy(ta_b[:], ta_sb[:].indirect(list_b[:]))
-        sums = [psum.tile([P, BANK], F32, name="sum%d" % c, tag="first%d" % c) for c in range(CHUNKS)]
+
+        sums = [psum.tile([P, BANK], F32, name="sum%d" % c, tag="bank%d" % (0, 1, 6, 7)[c]) for c in range(CHUNKS)]
 
         def add_turned(source, c, first, last):
             for b in range(BLOCKS):
@@ -167,57 +187,75 @@ def tile_attend_hvjointcover_heads_kernel(tc, hid, voc_words, voc_scales, stake,
         for c in range(CHUNKS):
             add_turned(base_sb[:, chunk(c)], c, True, False)
 
-        prods = column("prods", 2)
-        norm = column("norm")
-        nc.vector.scalar_tensor_tensor(prods[:], sums_f[:, 0:3:2], 1.0, sums_f[:, 0:2], mult, mult, accum_out=norm[:])
-        s_ab = prods[:, 1:2]
-        nc.vector.tensor_scalar(rows[:, 0:2, 0:KX], s_ba.unsqueeze(2).to_broadcast([P, 2, KX]), zq, -0.5, mult, mult)
-        nc.vector.tensor_scalar(rows[:, 2, KX:ROW], s_ba, zq, -4.0, mult, mult)
-        nc.vector.scalar_tensor_tensor(flat[:, KX : ROW + KX + 2 : ROW + 1], s_ba, -1.0, s_ba, mult, mult)
-        nc.vector.scalar_tensor_tensor(xp[:, 0:1024], ta_sb[:, 0:1024], 1.0, p[:, 0:1024], mult, mult, accum_out=xvec[:, 0:1])
-        rn = column("rn")
-        nc.vector.reciprocal(rn[:], norm[:])
-        nc.vector.tensor_scalar(sums_f[:, 3:4], s_ab, rq[:], -0.5, mult, mult)
-        t16 = column("t16")
-        nc.vector.tensor_scalar(t16[:], s_ab, rq[:], rq[:], mult, mult)
-        nc.vector.scalar_tensor_tensor(xp[:, 1024:2048], ta_sb[:, 1024:2048], 1.0, p[:, 1024:2048], mult, mult, accum_out=xvec[:, 1:2])
-        slope = column("slope", 3)
-        nc.vector.tensor_scalar(slope[:], sums_f[:, 1:4], rn[:], stake_k[:, 0:1], mult, mult)
-        gain = column("gain", 2)
-        nc.vector.tensor_scalar(gain[:], stake_k[:], rn[:], rn[:], mult, mult)
-        nc.vector.tensor_scalar(rows[:, 2, 0:KX], t16[:].to_broadcast([P, KX]), 3.0, s_ab, add, mult)
-        xpx_a = listed("xpx_a")
-        nc.vector.scalar_tensor_tensor(xpx_a[:], ta_a[:], 1.0, px_a[:], mult, mult, accum_out=xvec[:, KX : KX + 1])
-        xpx_b = listed("xpx_b")
-        nc.vector.scalar_tensor_tensor(xpx_b[:], ta_b[:], 1.0, px_b[:], mult, mult, accum_out=xvec[:, KX + 1 : ROW])
+        xpx_a, xpx_b = listed("xpx_a"), listed("xpx_b")
+        nc.vector.scalar_tensor_tensor(xpx_a[:], ta_a[:], stake_k[:, 1:2], px_a[:], mult, mult, accum_out=xvec[:, KX : KX + 1])
+        affine(divisors[:, 1:2], s_a, 1.0, 1e-27)
+        affine(divisors[:, 2:3], s_b, 1.0, 1e-27)
+        nc.vector.tensor_scalar(norm, s_b, s_a, zq2, mult, add)
+        cover = column("cover")
+        nc.vector.tensor_scalar(cover[:], s_b, s_a, stake_k[:, 2:3], mult, mult)
+        inverses = column("inverses", 4)
+        nc.vector.reciprocal(inverses[:], divisors[:])
+        rn, rq = inverses[:, 0:1], inverses[:, 3:4]
+        c1 = column("c1")
+        nc.vector.tensor_scalar(c1[:], cover[:], rn, rq, mult, mult)
+        slope = column("slope", 2)
+        nc.vector.tensor_scalar(slope[:], listed_sums[:], rn, stake_k[:, 0:1], mult, mult)
+        gain = column("gain")
+        nc.vector.tensor_scalar(gain[:], rn, rn, None, mult)
+        nc.vector.scalar_tensor_tensor(xpx_b[:], ta_b[:], stake_k[:, 1:2], px_b[:], mult, mult, accum_out=xvec[:, KX + 1 : ROW])
+        small = column("small", 2)
+        norm_zq2, norm_q = small[:, 0:1], small[:, 1:2]
+        scaled(z_half, z[:], 0.5)
+        scaled(z_eighth, z[:], 0.125)
+        scaled(flat[:, KX + 1 : ROW + KX + 1 : KX + 1], zq2.to_broadcast([P, 2]), -1.0)
+        nc.scalar.activation(flat[:, KX : ROW + KX + 2 : ROW + 1], listed_sums[:], ACT.Square)
+        scaled(norm_zq2, norm, zq2)
+        scaled(norm_q, norm, -0.25)
+        scaled(rows[:, 2, KX:ROW], listed_sums[:], z_eighth)
+        w = column("w")
+        affine(w[:], norm, rq, z_half)
+        scaled(rows[:, 0:2, 0:KX], inverses[:, 1:3].unsqueeze(2).to_broadcast([P, 2, KX]), norm_zq2)
+        scaled(rows[:, 2, 0:KX], w[:].to_broadcast([P, KX]), norm_q)
+        nc.vector.scalar_tensor_tensor(xp[:, 0:1024], ta_sb[:, 0:1024], c1[:], p[:, 0:1024], mult, mult, accum_out=xvec[:, 0:1])
+        for c in range(0, 2):
+            add_turned(xp[:, chunk(c)], c, False, False)
+        nc.vector.scalar_tensor_tensor(xp[:, 1024:2048], ta_sb[:, 1024:2048], c1[:], p[:, 1024:2048], mult, mult, accum_out=xvec[:, 1:2])
+        for c in range(2, 4):
+            add_turned(xp[:, chunk(c)], c, False, False)
+
         offset = column("offset", 3)
         terms = keep.tile([P, 3, ROW], F32, name="terms")
-        for k in range(3):
+
+        def row_offset(k):
             nc.vector.scalar_tensor_tensor(
-                terms[:, k, :], rows[:, k, :], gain[:, k // 2 : k // 2 + 1], xvec[:], mult, mult, accum_out=offset[:, k : k + 1]
+                terms[:, k, :], rows[:, k, :], gain[:], xvec[:], mult, mult, accum_out=offset[:, k : k + 1]
             )
 
         u_a, u_b = listed("u_a"), listed("u_b")
+        row_offset(0)
+        row_offset(2)
         nc.vector.tensor_scalar(u_a[:], ta_a[:], slope[:, 0:1], offset[:, 0:1], mult, add)
-        nc.vector.tensor_scalar(u_b[:], ta_b[:], slope[:, 1:2], offset[:, 1:2], mult, add)
+        row_offset(1)
         nc.vector.tensor_tensor(xs_a[:].indirect(list_a[:]), u_a[:], px_a[:], mult)
-        nc.vector.tensor_tensor(xs_b[:].indirect(list_b[:]), u_b[:], px_b[:], mult)
 
-        term_xp = [keep.tile([P, BANK], F32, name="term_xp%d" % c) for c in range(CHUNKS)]
         term_p = [keep.tile([P, BANK], F32, name="term_p%d" % c) for c in range(CHUNKS)]
-        for c in range(CHUNKS):
-            nc.scalar.activation(term_xp[c][:], xp[:, chunk(c)], ACT.Copy, scale=slope[:, 2:3])
-            add_turned(term_xp[c][:], c, False, False)
         for c in range(CHUNKS):
             nc.scalar.activation(term_p[c][:], p[:, chunk(c)], ACT.Copy, scale=offset[:, 2:3])
             add_turned(term_p[c][:], c, False, False)
+        affine(u_b[:], ta_b[:], slope[:, 1:2], offset[:, 1:2])
+        nc.vector.tensor_tensor(xs_b[:].indirect(list_b[:]), u_b[:], px_b[:], mult)
         for c in range(CHUNKS):
             add_turned(xs_a[:, chunk(c)], c, False, True)
+        for c in range(CHUNKS):
             turned = keep.tile([P, BANK], F32, name="turned%d" % c)
             nc.scalar.copy(turned[:], sums[c][:])
-            upright = psum.tile([P, BANK], F32, name="upright%d" % c, tag="second%d" % c)
+            upright = psum.tile([P, BANK], F32, name="upright%d" % c, tag="bank%d" % (4, 5, 2, 3)[c])
             for b in range(BLOCKS):
                 nc.tensor.transpose(upright[:, block(b)], turned[:, block(b)], ident[:])
-            result = keep.tile([P, BANK], F32, name="result%d" % c)
-            nc.vector.tensor_tensor(result[:], upright[:], xs_b[:, chunk(c)], add)
-            nc.sync.dma_start(out=out[:, chunk(c)], in_=result[:])
+            cuts = [[0, 128, 512], [0, 512], [0, 512], [0, 384, 512]][c]
+            for lo, hi in zip(cuts[:-1], cuts[1:]):
+                result = keep.tile([P, hi - lo], F32, name="result%d_%d" % (c, lo))
+                cols = slice(c * BANK + lo, c * BANK + hi)
+                nc.vector.tensor_tensor(result[:], upright[:, lo:hi], xs_b[:, cols], add)
+                nc.sync.dma_start(out=out[:, cols], in_=result[:])

@@ -17,9 +17,15 @@ AXIS = mybir.AxisListType
 P = 128
 D, V, Q, LISTED = 512, 2048, 128, 512
 PACK = 4
+QUADRANTS = 4
 BANK = 512
 CHUNKS = V // BANK
 BLOCKS = BANK // P
+HALVES = 2
+ROW = HALVES + 2
+XA, XB = HALVES, HALVES + 1
+TINY = 1e-27
+STORE_CUTS = ((0, P, BANK), (0, BANK), (0, BANK), (0, BANK - P, BANK))
 
 FLOPS = 2 * 2 * D * Q * V
 
@@ -41,6 +47,15 @@ def tile_attend_hvjointcover_heads_kernel(tc, hid, voc_words, voc_scales, stake,
         def column(name, width=1):
             return keep.tile([P, width], F32, name=name)
 
+        def listed(name):
+            return keep.tile([P, LISTED], F32, name=name)
+
+        def scaled(dst, src, scale):
+            nc.scalar.activation(dst, src, ACT.Copy, scale=scale)
+
+        def affine(dst, src, scale, bias):
+            nc.scalar.activation(dst, src, ACT.Identity, scale=scale, bias=bias)
+
         planes = keep.tile([P, BANK], U8, name="planes", align_bytes=64)
         nc.vector.memset(planes[:].bitcast(I32), 0)
 
@@ -48,9 +63,9 @@ def tile_attend_hvjointcover_heads_kernel(tc, hid, voc_words, voc_scales, stake,
         nc.sync.dma_start(out=hid_raw[:], in_=hid.rearrange("(p t) q -> p t q", t=PACK))
         dhid_raw = keep.tile([P, PACK, Q], F32, name="dhid_raw")
         nc.sync.dma_start(out=dhid_raw[:], in_=dhid.rearrange("(p t) q -> p t q", t=PACK))
-        for quad in range(4):
+        for quad in range(QUADRANTS):
             nc.sync.dma_start(
-                out=planes[32 * quad : 32 * quad + 16, :].bitcast(I32),
+                out=planes[32 * quad : 32 * quad + 4 * CHUNKS, :].bitcast(I32),
                 in_=voc_scales[0][4 * quad : 4 * quad + 4, :].bitcast(I32).rearrange("r (c n) -> c r n", c=CHUNKS),
             )
         words_hbm = voc_words[0].rearrange("p n t -> p (n t)")
@@ -69,10 +84,6 @@ def tile_attend_hvjointcover_heads_kernel(tc, hid, voc_words, voc_scales, stake,
         base_sb = keep.tile([P, V], F32, name="base_sb")
         nc.sync.dma_start(out=base_sb[:], in_=base)
 
-        warm = column("warm")
-        nc.vector.memset(warm[:], 0.0)
-        warm_out = column("warm_out")
-        nc.scalar.activation(warm_out[:], warm[:], ACT.Exp)
         ident = keep.tile([P, P], F32, name="ident")
         make_identity(nc, ident[:])
         xs_a = keep.tile([P, V], F32, name="xs_a")
@@ -122,56 +133,48 @@ def tile_attend_hvjointcover_heads_kernel(tc, hid, voc_words, voc_scales, stake,
 
         score(0)
         tangent(0, "bank4")
-        score(1)
-        score(2)
-        score(3)
+        for c in range(1, CHUNKS):
+            score(c)
         tangent(3, "bank5")
         tangent(1, "bank2")
         tangent(2, "bank3")
+        sum_banks = (0, 1, 6, 7)
+        upright_banks = (4, 5, 2, 3)
 
         neg_max = column("neg_max")
         nc.vector.tensor_reduce(neg_max[:], chunk_max[:], AXIS.X, ALU.max, negate=True)
 
-        def listed(name):
-            return keep.tile([P, LISTED], F32, name=name)
-
         a_a, a_b, ta_a, ta_b = listed("a_a"), listed("a_b"), listed("ta_a"), listed("ta_b")
         px_a, px_b = listed("px_a"), listed("px_b")
         p = keep.tile([P, V], F32, name="p")
-        xp = keep.tile([P, V], F32, name="xp")
+        term_xp = keep.tile([P, V], F32, name="xp")
         listed_sums = column("listed_sums", 2)
         s_b, s_a = listed_sums[:, 0:1], listed_sums[:, 1:2]
-        KX = 2
-        ROW = KX + 2
-        xvec = column("xvec", ROW)
-        rows = keep.tile([P, 3, ROW], F32, name="rows")
-        flat = rows[:].rearrange("p r k -> p (r k)")
-        def scaled(dst, src, scale):
-            nc.scalar.activation(dst, src, ACT.Copy, scale=scale)
-
-        def affine(dst, src, scale, bias):
-            nc.scalar.activation(dst, src, ACT.Identity, scale=scale, bias=bias)
+        row_sums = column("xvec", ROW)
+        factors = keep.tile([P, 3, ROW], F32, name="rows")
+        factors_flat = factors[:].rearrange("p r k -> p (r k)")
 
         stake_k = column("stake_k", 3)
-        for k, factor in enumerate((512.0, -512.0, -256.0)):
-            scaled(stake_k[:, k : k + 1], stake_sb[:], factor)
+        for j, factor in enumerate((512.0, -512.0, -256.0)):
+            scaled(stake_k[:, j : j + 1], stake_sb[:], factor)
+        k_plus, k_minus, k_minus_half = stake_k[:, 0:1], stake_k[:, 1:2], stake_k[:, 2:3]
         divisors = column("divisors", 4)
         norm, zq = divisors[:, 0:1], divisors[:, 3:4]
 
         nc.vector.tensor_copy(a_a[:], a_sb[:].indirect(list_a[:]))
         nc.vector.tensor_copy(a_b[:], a_sb[:].indirect(list_b[:]))
         z = column("z")
-        zs = column("zs", 3)
-        z_half, z_eighth, zq2 = zs[:, 0:1], zs[:, 1:2], zs[:, 2:3]
+        from_z = column("zs", 3)
+        zq_twice, zq_half, zq_squared = from_z[:, 0:1], from_z[:, 1:2], from_z[:, 2:3]
         nc.scalar.activation(p[:], a_sb[:], ACT.Exp, bias=neg_max[:], accum_out=z[:])
         nc.scalar.activation(px_a[:], a_a[:], ACT.Exp, bias=neg_max[:], accum_out=s_a)
-        nc.scalar.activation(zq2, z[:], ACT.Square, scale=0.25)
+        nc.scalar.activation(zq_squared, z[:], ACT.Square, scale=0.25)
         scaled(zq, z[:], 0.25)
         nc.scalar.activation(px_b[:], a_b[:], ACT.Exp, bias=neg_max[:], accum_out=s_b)
         nc.vector.tensor_copy(ta_a[:], ta_sb[:].indirect(list_a[:]))
         nc.vector.tensor_copy(ta_b[:], ta_sb[:].indirect(list_b[:]))
 
-        sums = [psum.tile([P, BANK], F32, name="sum%d" % c, tag="bank%d" % (0, 1, 6, 7)[c]) for c in range(CHUNKS)]
+        sums = [psum.tile([P, BANK], F32, name="sum%d" % c, tag="bank%d" % sum_banks[c]) for c in range(CHUNKS)]
 
         def add_turned(source, c, first, last):
             for b in range(BLOCKS):
@@ -188,73 +191,87 @@ def tile_attend_hvjointcover_heads_kernel(tc, hid, voc_words, voc_scales, stake,
             add_turned(base_sb[:, chunk(c)], c, True, False)
 
         xpx_a, xpx_b = listed("xpx_a"), listed("xpx_b")
-        nc.vector.scalar_tensor_tensor(xpx_a[:], ta_a[:], stake_k[:, 1:2], px_a[:], mult, mult, accum_out=xvec[:, KX : KX + 1])
-        affine(divisors[:, 1:2], s_a, 1.0, 1e-27)
-        affine(divisors[:, 2:3], s_b, 1.0, 1e-27)
-        nc.vector.tensor_scalar(norm, s_b, s_a, zq2, mult, add)
+        nc.vector.scalar_tensor_tensor(
+            xpx_a[:], ta_a[:], k_minus, px_a[:], mult, mult, accum_out=row_sums[:, XA : XA + 1]
+        )
+        affine(divisors[:, 1:2], s_a, 1.0, TINY)
+        affine(divisors[:, 2:3], s_b, 1.0, TINY)
+        nc.vector.tensor_scalar(norm, s_b, s_a, zq_squared, mult, add)
         cover = column("cover")
-        nc.vector.tensor_scalar(cover[:], s_b, s_a, stake_k[:, 2:3], mult, mult)
+        nc.vector.tensor_scalar(cover[:], s_b, s_a, k_minus_half, mult, mult)
         inverses = column("inverses", 4)
         nc.vector.reciprocal(inverses[:], divisors[:])
-        rn, rq = inverses[:, 0:1], inverses[:, 3:4]
+        inv_norm, inv_sums, inv_zq = inverses[:, 0:1], inverses[:, 1:3], inverses[:, 3:4]
         c1 = column("c1")
-        nc.vector.tensor_scalar(c1[:], cover[:], rn, rq, mult, mult)
+        nc.vector.tensor_scalar(c1[:], cover[:], inv_norm, inv_zq, mult, mult)
         slope = column("slope", 2)
-        nc.vector.tensor_scalar(slope[:], listed_sums[:], rn, stake_k[:, 0:1], mult, mult)
-        gain = column("gain")
-        nc.vector.tensor_scalar(gain[:], rn, rn, None, mult)
-        nc.vector.scalar_tensor_tensor(xpx_b[:], ta_b[:], stake_k[:, 1:2], px_b[:], mult, mult, accum_out=xvec[:, KX + 1 : ROW])
-        small = column("small", 2)
-        norm_zq2, norm_q = small[:, 0:1], small[:, 1:2]
-        scaled(z_half, z[:], 0.5)
-        scaled(z_eighth, z[:], 0.125)
-        scaled(flat[:, KX + 1 : ROW + KX + 1 : KX + 1], zq2.to_broadcast([P, 2]), -1.0)
-        nc.scalar.activation(flat[:, KX : ROW + KX + 2 : ROW + 1], listed_sums[:], ACT.Square)
-        scaled(norm_zq2, norm, zq2)
-        scaled(norm_q, norm, -0.25)
-        scaled(rows[:, 2, KX:ROW], listed_sums[:], z_eighth)
-        w = column("w")
-        affine(w[:], norm, rq, z_half)
-        scaled(rows[:, 0:2, 0:KX], inverses[:, 1:3].unsqueeze(2).to_broadcast([P, 2, KX]), norm_zq2)
-        scaled(rows[:, 2, 0:KX], w[:].to_broadcast([P, KX]), norm_q)
-        nc.vector.scalar_tensor_tensor(xp[:, 0:1024], ta_sb[:, 0:1024], c1[:], p[:, 0:1024], mult, mult, accum_out=xvec[:, 0:1])
-        for c in range(0, 2):
-            add_turned(xp[:, chunk(c)], c, False, False)
-        nc.vector.scalar_tensor_tensor(xp[:, 1024:2048], ta_sb[:, 1024:2048], c1[:], p[:, 1024:2048], mult, mult, accum_out=xvec[:, 1:2])
-        for c in range(2, 4):
-            add_turned(xp[:, chunk(c)], c, False, False)
+        nc.vector.tensor_scalar(slope[:], listed_sums[:], inv_norm, k_plus, mult, mult)
+        slope_a, slope_b = slope[:, 0:1], slope[:, 1:2]
+        inv_norm_squared = column("gain")
+        nc.vector.tensor_scalar(inv_norm_squared[:], inv_norm, inv_norm, None, mult)
+        nc.vector.scalar_tensor_tensor(
+            xpx_b[:], ta_b[:], k_minus, px_b[:], mult, mult, accum_out=row_sums[:, XB : XB + 1]
+        )
+        from_norm = column("small", 2)
+        norm_zq_squared, norm_quarter = from_norm[:, 0:1], from_norm[:, 1:2]
+        scaled(zq_twice, z[:], 0.5)
+        scaled(zq_half, z[:], 0.125)
+        scaled(factors_flat[:, XB : ROW + XA + 1 : ROW - 1], zq_squared.to_broadcast([P, 2]), -1.0)
+        nc.scalar.activation(factors_flat[:, XA : ROW + XB + 1 : ROW + 1], listed_sums[:], ACT.Square)
+        scaled(norm_zq_squared, norm, zq_squared)
+        scaled(norm_quarter, norm, -0.25)
+        scaled(factors[:, 2, XA:ROW], listed_sums[:], zq_half)
+        bracket = column("w")
+        affine(bracket[:], norm, inv_zq, zq_twice)
+        scaled(factors[:, 0:2, 0:HALVES], inv_sums.unsqueeze(2).to_broadcast([P, 2, HALVES]), norm_zq_squared)
+        scaled(factors[:, 2, 0:HALVES], bracket[:].to_broadcast([P, HALVES]), norm_quarter)
 
-        offset = column("offset", 3)
-        terms = keep.tile([P, 3, ROW], F32, name="terms")
-
-        def row_offset(k):
+        for half in range(HALVES):
+            cols = slice(half * V // HALVES, (half + 1) * V // HALVES)
             nc.vector.scalar_tensor_tensor(
-                terms[:, k, :], rows[:, k, :], gain[:], xvec[:], mult, mult, accum_out=offset[:, k : k + 1]
+                term_xp[:, cols], ta_sb[:, cols], c1[:], p[:, cols], mult, mult, accum_out=row_sums[:, half : half + 1]
+            )
+            for c in range(half * CHUNKS // HALVES, (half + 1) * CHUNKS // HALVES):
+                add_turned(term_xp[:, chunk(c)], c, False, False)
+
+        offsets = column("offset", 3)
+        e_a, e_b, c0 = offsets[:, 0:1], offsets[:, 1:2], offsets[:, 2:3]
+        summands = keep.tile([P, 3, ROW], F32, name="terms")
+
+        def dot_with_row_sums(j):
+            nc.vector.scalar_tensor_tensor(
+                summands[:, j, :],
+                factors[:, j, :],
+                inv_norm_squared[:],
+                row_sums[:],
+                mult,
+                mult,
+                accum_out=offsets[:, j : j + 1],
             )
 
         u_a, u_b = listed("u_a"), listed("u_b")
-        row_offset(0)
-        row_offset(2)
-        nc.vector.tensor_scalar(u_a[:], ta_a[:], slope[:, 0:1], offset[:, 0:1], mult, add)
-        row_offset(1)
+        dot_with_row_sums(0)
+        dot_with_row_sums(2)
+        nc.vector.tensor_scalar(u_a[:], ta_a[:], slope_a, e_a, mult, add)
+        dot_with_row_sums(1)
         nc.vector.tensor_tensor(xs_a[:].indirect(list_a[:]), u_a[:], px_a[:], mult)
 
         term_p = [keep.tile([P, BANK], F32, name="term_p%d" % c) for c in range(CHUNKS)]
         for c in range(CHUNKS):
-            nc.scalar.activation(term_p[c][:], p[:, chunk(c)], ACT.Copy, scale=offset[:, 2:3])
+            scaled(term_p[c][:], p[:, chunk(c)], c0)
             add_turned(term_p[c][:], c, False, False)
-        affine(u_b[:], ta_b[:], slope[:, 1:2], offset[:, 1:2])
+        affine(u_b[:], ta_b[:], slope_b, e_b)
         nc.vector.tensor_tensor(xs_b[:].indirect(list_b[:]), u_b[:], px_b[:], mult)
+
         for c in range(CHUNKS):
             add_turned(xs_a[:, chunk(c)], c, False, True)
         for c in range(CHUNKS):
             turned = keep.tile([P, BANK], F32, name="turned%d" % c)
             nc.scalar.copy(turned[:], sums[c][:])
-            upright = psum.tile([P, BANK], F32, name="upright%d" % c, tag="bank%d" % (4, 5, 2, 3)[c])
+            upright = psum.tile([P, BANK], F32, name="upright%d" % c, tag="bank%d" % upright_banks[c])
             for b in range(BLOCKS):
                 nc.tensor.transpose(upright[:, block(b)], turned[:, block(b)], ident[:])
-            cuts = [[0, 128, 512], [0, 512], [0, 512], [0, 384, 512]][c]
-            for lo, hi in zip(cuts[:-1], cuts[1:]):
+            for lo, hi in zip(STORE_CUTS[c][:-1], STORE_CUTS[c][1:]):
                 result = keep.tile([P, hi - lo], F32, name="result%d_%d" % (c, lo))
                 cols = slice(c * BANK + lo, c * BANK + hi)
                 nc.vector.tensor_tensor(result[:], upright[:, lo:hi], xs_b[:, cols], add)

from contextlib import ExitStack

import concourse.mybir as mybir
from concourse.masks import make_identity

F32 = mybir.dt.float32
BF16 = mybir.dt.bfloat16
I32 = mybir.dt.int32
U32 = mybir.dt.uint32
U16 = mybir.dt.uint16
U8 = mybir.dt.uint8
FP8X4 = mybir.dt.float8_e4m3fn_x4
ALU = mybir.AluOpType
ACT = mybir.ActivationFunctionType
AXIS = mybir.AxisListType

P = 128
D, V, Q, LISTED = 512, 2048, 128, 512
PACK = 4
QUADRANTS = 4
BANK = 512
CHUNKS = V // BANK
BLOCKS = BANK // P
HALVES = 2
ROW = HALVES + 2
XA, XB = HALVES, HALVES + 1
TINY = 1e-27
STORE_CUTS = ((0, P, BANK), (0, BANK), (0, BANK), (0, BANK - P, BANK))

FLOPS = 2 * 2 * D * Q * V


def tile_attend_hvjointcover_heads_kernel(tc, hid, voc_words, voc_scales, stake, dhid, base, offs, offs2, out):
    nc = tc.nc
    mult, add = ALU.mult, ALU.add

    with ExitStack() as ctx:
        keep = ctx.enter_context(tc.tile_pool(name="keep", bufs=1))
        psum = ctx.enter_context(tc.psum_pool(name="psum", bufs=1))

        def chunk(c):
            return slice(c * BANK, (c + 1) * BANK)

        def block(b):
            return slice(b * P, (b + 1) * P)

        def column(name, width=1):
            return keep.tile([P, width], F32, name=name)

        def listed(name):
            return keep.tile([P, LISTED], F32, name=name)

        def scaled(dst, src, scale):
            nc.scalar.activation(dst, src, ACT.Copy, scale=scale)

        def affine(dst, src, scale, bias):
            nc.scalar.activation(dst, src, ACT.Identity, scale=scale, bias=bias)

        planes = keep.tile([P, BANK], U8, name="planes", align_bytes=64)
        nc.vector.memset(planes[:].bitcast(I32), 0)

        hid_raw = keep.tile([P, PACK, Q], F32, name="hid_raw")
        nc.sync.dma_start(out=hid_raw[:], in_=hid.rearrange("(p t) q -> p t q", t=PACK))
        dhid_raw = keep.tile([P, PACK, Q], F32, name="dhid_raw")
        nc.sync.dma_start(out=dhid_raw[:], in_=dhid.rearrange("(p t) q -> p t q", t=PACK))
        for quad in range(QUADRANTS):
            nc.sync.dma_start(
                out=planes[32 * quad : 32 * quad + 4 * CHUNKS, :].bitcast(I32),
                in_=voc_scales[0][4 * quad : 4 * quad + 4, :].bitcast(I32).rearrange("r (c n) -> c r n", c=CHUNKS),
            )
        words_hbm = voc_words[0].rearrange("p n t -> p (n t)")
        words = [keep.tile([P, BANK], U32, name="words%d" % c, align_bytes=64) for c in range(CHUNKS)]
        for c in range(CHUNKS):
            nc.sync.dma_start(
                out=words[c][:].bitcast(I32),
                in_=words_hbm[:, PACK * c * BANK : PACK * (c + 1) * BANK].bitcast(I32),
            )
        list_a = keep.tile([P, LISTED // 16], U16, name="list_a")
        list_b = keep.tile([P, LISTED // 16], U16, name="list_b")
        nc.sync.dma_start(list_a[:], offs)
        nc.sync.dma_start(list_b[:], offs2)
        stake_sb = column("stake_sb")
        nc.sync.dma_start(out=stake_sb[:], in_=stake)
        base_sb = keep.tile([P, V], F32, name="base_sb")
        nc.sync.dma_start(out=base_sb[:], in_=base)

        ident = keep.tile([P, P], F32, name="ident")
        make_identity(nc, ident[:])
        xs_a = keep.tile([P, V], F32, name="xs_a")
        nc.vector.memset(xs_a[:], 0.0)

        def quantise(raw, name, tag, cast):
            grouped = keep.tile([P, Q, PACK], BF16, name=name + "_bf16", tag=tag, align_bytes=64)
            cast(grouped[:], raw[:].rearrange("p t q -> p q t"))
            codes = keep.tile([P, Q], U32, name=name + "_codes", align_bytes=64)
            scales = keep.tile([P, Q], U8, name=name + "_scales", align_bytes=64)
            nc.vector.quantize_mx(
                out=codes[:].bitcast(FP8X4), scales=scales[:], in_=grouped[:].rearrange("p q t -> p (q t)")
            )
            return codes, scales

        hid_mx = quantise(hid_raw, "hid", "hid_bf16", nc.vector.tensor_copy)
        dhid_mx = quantise(dhid_raw, "dhid", "late", nc.scalar.copy)
        xs_b = keep.tile([P, V], F32, name="xs_b", tag="late", align_bytes=64)
        nc.gpsimd.memset(xs_b[:], 0.0)

        a_sb = keep.tile([P, V], F32, name="a_sb")
        ta_sb = keep.tile([P, V], F32, name="ta_sb")
        chunk_max = column("chunk_max", CHUNKS)

        def product(operand, c, tag):
            bank = psum.tile([P, BANK], F32, name=tag + "_mx", tag=tag)
            nc.tensor.matmul_mx(
                out=bank[:],
                lhsT=operand[0][:].bitcast(FP8X4),
                lhsT_scale=operand[1][:],
                rhs=words[c][:].bitcast(FP8X4),
                rhs_scale=planes[4 * c : P, :],
                start=True,
                stop=True,
            )
            return bank

        def score(c):
            bank = product(hid_mx, c, "bank%d" % c)
            nc.vector.tensor_scalar(
                a_sb[:, chunk(c)], bank[:], 1.0, None, mult, ALU.max, accum_out=chunk_max[:, c : c + 1]
            )

        def tangent(c, tag):
            bank = product(dhid_mx, c, tag)
            nc.scalar.copy(ta_sb[:, chunk(c)], bank[:])

        score(0)
        tangent(0, "bank4")
        for c in range(1, CHUNKS):
            score(c)
        tangent(3, "bank5")
        tangent(1, "bank2")
        tangent(2, "bank3")
        sum_banks = (0, 1, 6, 7)
        upright_banks = (4, 5, 2, 3)

        neg_max = column("neg_max")
        nc.vector.tensor_reduce(neg_max[:], chunk_max[:], AXIS.X, ALU.max, negate=True)

        a_a, a_b, ta_a, ta_b = listed("a_a"), listed("a_b"), listed("ta_a"), listed("ta_b")
        px_a, px_b = listed("px_a"), listed("px_b")
        p = keep.tile([P, V], F32, name="p")
        term_xp = keep.tile([P, V], F32, name="xp")
        listed_sums = column("listed_sums", 2)
        s_b, s_a = listed_sums[:, 0:1], listed_sums[:, 1:2]
        row_sums = column("xvec", ROW)
        factors = keep.tile([P, 3, ROW], F32, name="rows")
        factors_flat = factors[:].rearrange("p r k -> p (r k)")

        stake_k = column("stake_k", 3)
        for j, factor in enumerate((512.0, -512.0, -256.0)):
            scaled(stake_k[:, j : j + 1], stake_sb[:], factor)
        k_plus, k_minus, k_minus_half = stake_k[:, 0:1], stake_k[:, 1:2], stake_k[:, 2:3]
        divisors = column("divisors", 4)
        norm, zq = divisors[:, 0:1], divisors[:, 3:4]

        nc.vector.tensor_copy(a_a[:], a_sb[:].indirect(list_a[:]))
        nc.vector.tensor_copy(a_b[:], a_sb[:].indirect(list_b[:]))
        z = column("z")
        from_z = column("zs", 3)
        zq_twice, zq_half, zq_squared = from_z[:, 0:1], from_z[:, 1:2], from_z[:, 2:3]
        nc.scalar.activation(p[:], a_sb[:], ACT.Exp, bias=neg_max[:], accum_out=z[:])
        nc.scalar.activation(px_a[:], a_a[:], ACT.Exp, bias=neg_max[:], accum_out=s_a)
        nc.scalar.activation(zq_squared, z[:], ACT.Square, scale=0.25)
        scaled(zq, z[:], 0.25)
        nc.scalar.activation(px_b[:], a_b[:], ACT.Exp, bias=neg_max[:], accum_out=s_b)
        nc.vector.tensor_copy(ta_a[:], ta_sb[:].indirect(list_a[:]))
        nc.vector.tensor_copy(ta_b[:], ta_sb[:].indirect(list_b[:]))

        sums = [psum.tile([P, BANK], F32, name="sum%d" % c, tag="bank%d" % sum_banks[c]) for c in range(CHUNKS)]

        def add_turned(source, c, first, last):
            for b in range(BLOCKS):
                nc.tensor.matmul(
                    sums[c][:, block(b)],
                    lhsT=source[:, block(b)],
                    rhs=ident[:],
                    start=(first and b == 0),
                    stop=(last and b == BLOCKS - 1),
                    is_transpose=True,
                )

        for c in range(CHUNKS):
            add_turned(base_sb[:, chunk(c)], c, True, False)

        xpx_a, xpx_b = listed("xpx_a"), listed("xpx_b")
        nc.vector.scalar_tensor_tensor(
            xpx_a[:], ta_a[:], k_minus, px_a[:], mult, mult, accum_out=row_sums[:, XA : XA + 1]
        )
        affine(divisors[:, 1:2], s_a, 1.0, TINY)
        affine(divisors[:, 2:3], s_b, 1.0, TINY)
        nc.vector.tensor_scalar(norm, s_b, s_a, zq_squared, mult, add)
        cover = column("cover")
        nc.vector.tensor_scalar(cover[:], s_b, s_a, k_minus_half, mult, mult)
        inverses = column("inverses", 4)
        nc.vector.reciprocal(inverses[:], divisors[:])
        inv_norm, inv_sums, inv_zq = inverses[:, 0:1], inverses[:, 1:3], inverses[:, 3:4]
        c1 = column("c1")
        nc.vector.tensor_scalar(c1[:], cover[:], inv_norm, inv_zq, mult, mult)
        slope = column("slope", 2)
        nc.vector.tensor_scalar(slope[:], listed_sums[:], inv_norm, k_plus, mult, mult)
        slope_a, slope_b = slope[:, 0:1], slope[:, 1:2]
        inv_norm_squared = column("gain")
        nc.vector.tensor_scalar(inv_norm_squared[:], inv_norm, inv_norm, None, mult)
        nc.vector.scalar_tensor_tensor(
            xpx_b[:], ta_b[:], k_minus, px_b[:], mult, mult, accum_out=row_sums[:, XB : XB + 1]
        )
        from_norm = column("small", 2)
        norm_zq_squared, norm_quarter = from_norm[:, 0:1], from_norm[:, 1:2]
        scaled(zq_twice, z[:], 0.5)
        scaled(zq_half, z[:], 0.125)
        scaled(factors_flat[:, XB : ROW + XA + 1 : ROW - 1], zq_squared.to_broadcast([P, 2]), -1.0)
        nc.scalar.activation(factors_flat[:, XA : ROW + XB + 1 : ROW + 1], listed_sums[:], ACT.Square)
        scaled(norm_zq_squared, norm, zq_squared)
        scaled(norm_quarter, norm, -0.25)
        scaled(factors[:, 2, XA:ROW], listed_sums[:], zq_half)
        bracket = column("w")
        affine(bracket[:], norm, inv_zq, zq_twice)
        scaled(factors[:, 0:2, 0:HALVES], inv_sums.unsqueeze(2).to_broadcast([P, 2, HALVES]), norm_zq_squared)
        scaled(factors[:, 2, 0:HALVES], bracket[:].to_broadcast([P, HALVES]), norm_quarter)

        for half in range(HALVES):
            cols = slice(half * V // HALVES, (half + 1) * V // HALVES)
            nc.vector.scalar_tensor_tensor(
                term_xp[:, cols], ta_sb[:, cols], c1[:], p[:, cols], mult, mult, accum_out=row_sums[:, half : half + 1]
            )
            for c in range(half * CHUNKS // HALVES, (half + 1) * CHUNKS // HALVES):
                add_turned(term_xp[:, chunk(c)], c, False, False)

        offsets = column("offset", 3)
        e_a, e_b, c0 = offsets[:, 0:1], offsets[:, 1:2], offsets[:, 2:3]
        summands = keep.tile([P, 3, ROW], F32, name="terms")

        def dot_with_row_sums(j):
            nc.vector.scalar_tensor_tensor(
                summands[:, j, :],
                factors[:, j, :],
                inv_norm_squared[:],
                row_sums[:],
                mult,
                mult,
                accum_out=offsets[:, j : j + 1],
            )

        u_a, u_b = listed("u_a"), listed("u_b")
        dot_with_row_sums(0)
        dot_with_row_sums(2)
        nc.vector.tensor_scalar(u_a[:], ta_a[:], slope_a, e_a, mult, add)
        dot_with_row_sums(1)
        nc.vector.tensor_tensor(xs_a[:].indirect(list_a[:]), u_a[:], px_a[:], mult)

        term_p = [keep.tile([P, BANK], F32, name="term_p%d" % c) for c in range(CHUNKS)]
        for c in range(CHUNKS):
            scaled(term_p[c][:], p[:, chunk(c)], c0)
            add_turned(term_p[c][:], c, False, False)
        affine(u_b[:], ta_b[:], slope_b, e_b)
        nc.vector.tensor_tensor(xs_b[:].indirect(list_b[:]), u_b[:], px_b[:], mult)

        for c in range(CHUNKS):
            add_turned(xs_a[:, chunk(c)], c, False, True)
        for c in range(CHUNKS):
            turned = keep.tile([P, BANK], F32, name="turned%d" % c)
            nc.scalar.copy(turned[:], sums[c][:])
            upright = psum.tile([P, BANK], F32, name="upright%d" % c, tag="bank%d" % upright_banks[c])
            for b in range(BLOCKS):
                nc.tensor.transpose(upright[:, block(b)], turned[:, block(b)], ident[:])
            for lo, hi in zip(STORE_CUTS[c][:-1], STORE_CUTS[c][1:]):
                result = keep.tile([P, hi - lo], F32, name="result%d_%d" % (c, lo))
                cols = slice(c * BANK + lo, c * BANK + hi)
                nc.vector.tensor_tensor(result[:], upright[:, lo:hi], xs_b[:, cols], add)
                nc.sync.dma_start(out=out[:, cols], in_=result[:])
